import numpy as np, ml_dtypes
CORES = [0,1,2,3,4,5,6,7,8,9,10,11,12,13,14,15,128,129,130,131,132,133,134,135,136,137,138,139,140,141,142,143]
N = 32
ROOT = 21
def setup_inputs(rng):
    return {"x": rng.standard_normal((N, 128, 1024), dtype=np.float32).astype(ml_dtypes.bfloat16)}
def reference(x):
    return {"y": np.broadcast_to(x[ROOT], x.shape)}

@@ -1,0 +1,78 @@
+from concourse.bass import DstId, RemoteDMATransfer
+
+NPIECE = 8
+SCRATCH = {
+    "d": ("dram", [NPIECE, 128, 128], "bfloat16"),
+}
+SEMAPHORES = ["ld", "seed", "glo", "ghi", "sent", "slo", "shi"]
+
+PORT = (2, 3, 6, 7)
+
+
+def rank_program(g, core, T, topo):
+    if T.rank_of(core) is None:
+        return
+    S = T.sem
+    root = T.cores[T.root]
+    A = root - root % 8
+    B, C, D = A ^ 8, A ^ 128, A ^ 136
+    base, me = core - core % 8, core % 8
+
+    def gsem(e):
+        return S.glo if e < 4 else S.ghi
+
+    def tr(e, dsts, lo, n, sem):
+        ids = []
+        for c in dsts:
+            rid, pid = topo.addr(c, core)
+            ids.append(DstId(rid=rid, pnc=pid))
+        return RemoteDMATransfer(dst_ids=ids, dma_engine_mask=((1 << n) - 1) << lo, remote_sem=sem,
+                                 srcs=[T.d[e]], dsts=[T.d[e] for c in dsts])
+
+    def stores(seed, lo, hi, mine):
+        for q, sem, cnt, done, half in ((g.sync, S.glo, lo, S.slo, 0), (g.scalar, S.ghi, hi, S.shi, 1)):
+            if seed and [e for e in mine if e // 4 == half]:
+                q.wait_ge(S.seed, seed)
+            if cnt:
+                q.wait_ge(sem, cnt)
+            q.dma_start(T.y[64 * half:64 * half + 64, :], T.d[4 * half:4 * half + 4]).then_inc(done, 16)
+            q.wait_ge(done, 16)
+
+    if core == root:
+        g.sync.dma_start(T.d[:], T.x[:]).then_inc(S.ld, 16)
+        g.wait_ge(S.ld, 16)
+        g.remote_dma_fused([tr(e, [A + PORT[e // 2]], 2 * e, 2, S.seed) for e in range(NPIECE)], local_sem=S.sent)
+        g.remote_dma_fused([tr(e, [C + e], e, 1, S.seed) for e in range(NPIECE)]
+                           + [tr(e, [A + 4], 8 + e, 1, gsem(e)) for e in range(NPIECE)], local_sem=S.sent)
+        g.scalar.wait_ge(S.sent, 32)
+        g.scalar.dma_start(T.y[:], T.x[:]).then_inc(S.shi, 16)
+        g.scalar.wait_ge(S.shi, 16)
+        g.wait_ge(S.sent, 32)
+        return
+
+    if base == A:
+        if me in PORT:
+            q = PORT.index(me)
+            a, b = 2 * q, 2 * q + 1
+            ring = [A + c for c in (0, 2, 6, 1, 3, 7)]
+            k = ring.index(core)
+            near = ring[k + 1:] + ring[:k]
+            g.wait_ge(S.seed, 4)
+            g.remote_dma_fused([tr(a, [D + a, B + a], 0, 4, S.seed), tr(b, [D + b, B + b], 4, 4, S.seed),
+                                tr(a, near, 8, 4, gsem(a)), tr(b, near, 12, 4, gsem(b))], local_sem=S.sent)
+            stores(4, 8 if q < 2 else 16, 16 if q < 2 else 8, (a, b))
+            g.wait_ge(S.sent, 16)
+        elif me == 4:
+            stores(0, 4, 4, ())
+        else:
+            stores(0, 16, 16, ())
+        return
+
+    seed = 1 if base == C else 4
+    h = me // 4
+    own = [base + 4 * h + (me + i) % 4 for i in range(1, 4)]
+    far = [base + 4 * (1 - h) + (me + i) % 4 for i in range(4)]
+    g.wait_ge(S.seed, seed)
+    g.remote_dma_fused([tr(me, own + far, 0, 16, gsem(me))], local_sem=S.sent)
+    stores(seed, 48 if h == 0 else 64, 64 if h == 0 else 48, (me,))
+    g.wait_ge(S.sent, 16)

@@ -1,10 +1,9 @@
 from concourse.bass import DstId, RemoteDMATransfer
 
-NPIECE = 8
 SCRATCH = {
-    "d": ("dram", [NPIECE, 128, 128], "bfloat16"),
+    "d": ("dram", [8, 128, 128], "bfloat16"),
 }
-SEMAPHORES = ["ld", "seed", "glo", "ghi", "sent", "slo", "shi"]
+SEMAPHORES = ["ld", "seed", "glo", "ghi", "gp0", "gp1", "gp2", "gp3", "sent", "slo", "shi"]
 
 PORT = (2, 3, 6, 7)
 
@@ -33,17 +32,16 @@ def rank_program(g, core, T, topo):
         for q, sem, cnt, done, half in ((g.sync, S.glo, lo, S.slo, 0), (g.scalar, S.ghi, hi, S.shi, 1)):
             if seed and [e for e in mine if e // 4 == half]:
                 q.wait_ge(S.seed, seed)
-            if cnt:
-                q.wait_ge(sem, cnt)
+            q.wait_ge(sem, cnt)
             q.dma_start(T.y[64 * half:64 * half + 64, :], T.d[4 * half:4 * half + 4]).then_inc(done, 16)
             q.wait_ge(done, 16)
 
     if core == root:
         g.sync.dma_start(T.d[:], T.x[:]).then_inc(S.ld, 16)
         g.wait_ge(S.ld, 16)
-        g.remote_dma_fused([tr(e, [A + PORT[e // 2]], 2 * e, 2, S.seed) for e in range(NPIECE)], local_sem=S.sent)
-        g.remote_dma_fused([tr(e, [C + e], e, 1, S.seed) for e in range(NPIECE)]
-                           + [tr(e, [A + 4], 8 + e, 1, gsem(e)) for e in range(NPIECE)], local_sem=S.sent)
+        g.remote_dma_fused([tr(e, [A + PORT[e // 2]], 2 * e, 2, S.seed) for e in range(8)], local_sem=S.sent)
+        g.remote_dma_fused([tr(e, [C + e], e, 1, S.seed) for e in range(8)]
+                           + [tr(e, [A + 4], 8 + e, 1, gsem(e)) for e in range(8)], local_sem=S.sent)
         g.scalar.wait_ge(S.sent, 32)
         g.scalar.dma_start(T.y[:], T.x[:]).then_inc(S.shi, 16)
         g.scalar.wait_ge(S.shi, 16)
@@ -69,10 +67,17 @@ def rank_program(g, core, T, topo):
         return
 
     seed = 1 if base == C else 4
-    h = me // 4
-    own = [base + 4 * h + (me + i) % 4 for i in range(1, 4)]
-    far = [base + 4 * (1 - h) + (me + i) % 4 for i in range(4)]
+    order = [base + (me ^ i) for i in (1, 2, 3, 4, 5, 6, 7)]
+    mp = me // 2
     g.wait_ge(S.seed, seed)
-    g.remote_dma_fused([tr(me, own + far, 0, 16, gsem(me))], local_sem=S.sent)
-    stores(seed, 48 if h == 0 else 64, 64 if h == 0 else 48, (me,))
+    g.remote_dma_fused([tr(me, order, 0, 16, S["gp" + str(mp)])], local_sem=S.sent)
+    for k in range(4):
+        p = mp ^ k
+        q, done = ((g.sync, S.slo), (g.scalar, S.shi))[k % 2]
+        if k == 0:
+            q.wait_ge(S.seed, seed)
+        q.wait_ge(S["gp" + str(p)], 16 if k == 0 else 32)
+        q.dma_start(T.y[32 * p:32 * p + 32, :], T.d[2 * p:2 * p + 2]).then_inc(done, 16)
+    g.sync.wait_ge(S.slo, 32)
+    g.scalar.wait_ge(S.shi, 32)
     g.wait_ge(S.sent, 16)

@@ -3,9 +3,10 @@ from concourse.bass import DstId, RemoteDMATransfer
 SCRATCH = {
     "d": ("dram", [8, 128, 128], "bfloat16"),
 }
-SEMAPHORES = ["ld", "seed", "glo", "ghi", "gp0", "gp1", "gp2", "gp3", "sent", "slo", "shi"]
+SEMAPHORES = ["ld", "go", "rs", "hlo", "hhi", "gp0", "gp1", "gp2", "gp3", "sent", "slo", "shi"]
 
 PORT = (2, 3, 6, 7)
+NEAR = {2: ((0, 1, 3, 6), (4, 7)), 3: ((1, 0, 2, 7), (4, 6)), 6: ((4, 0, 7, 2), (1, 3)), 7: ((1, 4, 6, 3), (0, 2))}
 
 
 def rank_program(g, core, T, topo):
@@ -17,9 +18,6 @@ def rank_program(g, core, T, topo):
     B, C, D = A ^ 8, A ^ 128, A ^ 136
     base, me = core - core % 8, core % 8
 
-    def gsem(e):
-        return S.glo if e < 4 else S.ghi
-
     def tr(e, dsts, lo, n, sem):
         ids = []
         for c in dsts:
@@ -28,54 +26,54 @@ def rank_program(g, core, T, topo):
         return RemoteDMATransfer(dst_ids=ids, dma_engine_mask=((1 << n) - 1) << lo, remote_sem=sem,
                                  srcs=[T.d[e]], dsts=[T.d[e] for c in dsts])
 
-    def stores(seed, lo, hi, mine):
-        for q, sem, cnt, done, half in ((g.sync, S.glo, lo, S.slo, 0), (g.scalar, S.ghi, hi, S.shi, 1)):
-            if seed and [e for e in mine if e // 4 == half]:
-                q.wait_ge(S.seed, seed)
-            q.wait_ge(sem, cnt)
+    def stores(lo_waits, hi_waits):
+        for q, waits, done, half in ((g.sync, lo_waits, S.slo, 0), (g.scalar, hi_waits, S.shi, 1)):
+            for sem, cnt in waits:
+                q.wait_ge(sem, cnt)
             q.dma_start(T.y[64 * half:64 * half + 64, :], T.d[4 * half:4 * half + 4]).then_inc(done, 16)
             q.wait_ge(done, 16)
 
     if core == root:
         g.sync.dma_start(T.d[:], T.x[:]).then_inc(S.ld, 16)
         g.wait_ge(S.ld, 16)
-        g.remote_dma_fused([tr(e, [A + PORT[e // 2]], 2 * e, 2, S.seed) for e in range(8)], local_sem=S.sent)
-        g.remote_dma_fused([tr(e, [C + e], e, 1, S.seed) for e in range(8)]
-                           + [tr(e, [A + 4], 8 + e, 1, gsem(e)) for e in range(8)], local_sem=S.sent)
-        g.scalar.wait_ge(S.sent, 32)
+        g.remote_dma_fused([tr(e, [A + PORT[e // 2]], 2 * e, 2, S.rs) for e in range(8)], local_sem=S.sent)
+        g.remote_dma_fused([tr(e, [C + e], e, 1, S.rs) for e in range(8)], local_sem=S.sent)
+        g.sem_inc(S.go, 1)
+        g.scalar.wait_ge(S.go, 1)
         g.scalar.dma_start(T.y[:], T.x[:]).then_inc(S.shi, 16)
         g.scalar.wait_ge(S.shi, 16)
-        g.wait_ge(S.sent, 32)
+        g.wait_ge(S.sent, 24)
         return
 
     if base == A:
         if me in PORT:
-            q = PORT.index(me)
-            a, b = 2 * q, 2 * q + 1
-            ring = [A + c for c in (0, 2, 6, 1, 3, 7)]
-            k = ring.index(core)
-            near = ring[k + 1:] + ring[:k]
-            g.wait_ge(S.seed, 4)
-            g.remote_dma_fused([tr(a, [D + a, B + a], 0, 4, S.seed), tr(b, [D + b, B + b], 4, 4, S.seed),
-                                tr(a, near, 8, 4, gsem(a)), tr(b, near, 12, 4, gsem(b))], local_sem=S.sent)
-            stores(4, 8 if q < 2 else 16, 16 if q < 2 else 8, (a, b))
+            a = 2 * PORT.index(me)
+            b = a + 1
+            h = S.hlo if a < 4 else S.hhi
+            ring = [A + c for c in NEAR[me][0]]
+            tail = [A + c for c in NEAR[me][1]]
+            g.wait_ge(S.rs, 4)
+            g.remote_dma_fused([tr(a, [D + a, B + a] + tail, 0, 4, h), tr(b, [D + b, B + b] + tail, 4, 4, h),
+                                tr(a, ring, 8, 4, h), tr(b, ring, 12, 4, h)], local_sem=S.sent)
+            if a < 4:
+                stores([(S.rs, 4), (S.hlo, 8)], [(S.hhi, 16)])
+            else:
+                stores([(S.hlo, 16)], [(S.rs, 4), (S.hhi, 8)])
             g.wait_ge(S.sent, 16)
-        elif me == 4:
-            stores(0, 4, 4, ())
         else:
-            stores(0, 16, 16, ())
+            stores([(S.hlo, 16)], [(S.hhi, 16)])
         return
 
-    seed = 1 if base == C else 4
+    seed = (S.rs, 1) if base == C else ((S.hlo, S.hhi)[me // 4], 4)
     order = [base + (me ^ i) for i in (1, 2, 3, 4, 5, 6, 7)]
     mp = me // 2
-    g.wait_ge(S.seed, seed)
+    g.wait_ge(seed[0], seed[1])
     g.remote_dma_fused([tr(me, order, 0, 16, S["gp" + str(mp)])], local_sem=S.sent)
     for k in range(4):
         p = mp ^ k
         q, done = ((g.sync, S.slo), (g.scalar, S.shi))[k % 2]
         if k == 0:
-            q.wait_ge(S.seed, seed)
+            q.wait_ge(seed[0], seed[1])
         q.wait_ge(S["gp" + str(p)], 16 if k == 0 else 32)
         q.dma_start(T.y[32 * p:32 * p + 32, :], T.d[2 * p:2 * p + 2]).then_inc(done, 16)
     g.sync.wait_ge(S.slo, 32)

from concourse.bass import DstId, RemoteDMATransfer

SCRATCH = {
    "d": ("dram", [8, 128, 128], "bfloat16"),
}
SEMAPHORES = ["ld", "go", "rs", "hlo", "hhi", "gp0", "gp1", "gp2", "gp3", "sent", "slo", "shi"]

PORT = (2, 3, 6, 7)
NEAR = {2: ((0, 1, 3, 6), (4, 7)), 3: ((1, 0, 2, 7), (4, 6)), 6: ((4, 0, 7, 2), (1, 3)), 7: ((1, 4, 6, 3), (0, 2))}


def rank_program(g, core, T, topo):
    if T.rank_of(core) is None:
        return
    S = T.sem
    root = T.cores[T.root]
    A = root - root % 8
    B, C, D = A ^ 8, A ^ 128, A ^ 136
    base, me = core - core % 8, core % 8

    def tr(e, dsts, lo, n, sem):
        ids = []
        for c in dsts:
            rid, pid = topo.addr(c, core)
            ids.append(DstId(rid=rid, pnc=pid))
        return RemoteDMATransfer(dst_ids=ids, dma_engine_mask=((1 << n) - 1) << lo, remote_sem=sem,
                                 srcs=[T.d[e]], dsts=[T.d[e] for c in dsts])

    def stores(lo_waits, hi_waits):
        for q, waits, done, half in ((g.sync, lo_waits, S.slo, 0), (g.scalar, hi_waits, S.shi, 1)):
            for sem, cnt in waits:
                q.wait_ge(sem, cnt)
            q.dma_start(T.y[64 * half:64 * half + 64, :], T.d[4 * half:4 * half + 4]).then_inc(done, 16)
            q.wait_ge(done, 16)

    if core == root:
        g.sync.dma_start(T.d[:], T.x[:]).then_inc(S.ld, 16)
        g.wait_ge(S.ld, 16)
        g.remote_dma_fused([tr(e, [A + PORT[e // 2]], 2 * e, 2, S.rs) for e in range(8)], local_sem=S.sent)
        g.remote_dma_fused([tr(e, [C + e], e, 1, S.rs) for e in range(8)], local_sem=S.sent)
        g.sem_inc(S.go, 1)
        g.scalar.wait_ge(S.go, 1)
        g.scalar.dma_start(T.y[:], T.x[:]).then_inc(S.shi, 16)
        g.scalar.wait_ge(S.shi, 16)
        g.wait_ge(S.sent, 24)
        return

    if base == A:
        if me in PORT:
            a = 2 * PORT.index(me)
            b = a + 1
            h = S.hlo if a < 4 else S.hhi
            ring = [A + c for c in NEAR[me][0]]
            tail = [A + c for c in NEAR[me][1]]
            g.wait_ge(S.rs, 4)
            g.remote_dma_fused([tr(a, [D + a, B + a] + tail, 0, 4, h), tr(b, [D + b, B + b] + tail, 4, 4, h),
                                tr(a, ring, 8, 4, h), tr(b, ring, 12, 4, h)], local_sem=S.sent)
            if a < 4:
                stores([(S.rs, 4), (S.hlo, 8)], [(S.hhi, 16)])
            else:
                stores([(S.hlo, 16)], [(S.rs, 4), (S.hhi, 8)])
            g.wait_ge(S.sent, 16)
        else:
            stores([(S.hlo, 16)], [(S.hhi, 16)])
        return

    seed = (S.rs, 1) if base == C else ((S.hlo, S.hhi)[me // 4], 4)
    order = [base + (me ^ i) for i in (1, 2, 3, 4, 5, 6, 7)]
    mp = me // 2
    g.wait_ge(seed[0], seed[1])
    g.remote_dma_fused([tr(me, order, 0, 16, S["gp" + str(mp)])], local_sem=S.sent)
    for k in range(4):
        p = mp ^ k
        q, done = ((g.sync, S.slo), (g.scalar, S.shi))[k % 2]
        if k == 0:
            q.wait_ge(seed[0], seed[1])
        q.wait_ge(S["gp" + str(p)], 16 if k == 0 else 32)
        q.dma_start(T.y[32 * p:32 * p + 32, :], T.d[2 * p:2 * p + 2]).then_inc(done, 16)
    g.sync.wait_ge(S.slo, 32)
    g.scalar.wait_ge(S.shi, 32)
    g.wait_ge(S.sent, 16)
